import numpy as np
import ml_dtypes


def mxq(x, axis, fmt="e4m3"):
    dtype, down = {"e4m3": (ml_dtypes.float8_e4m3fn, 7), "e5m2": (ml_dtypes.float8_e5m2, 14)}[fmt]
    v = np.moveaxis(np.asarray(x, np.float32).astype(ml_dtypes.bfloat16).astype(np.float64), axis, -1)
    blocks = v.reshape(v.shape[:-1] + (-1, 32))
    amax = np.abs(blocks).max(-1, keepdims=True)
    byte = np.maximum(np.where(amax > 0, np.frexp(amax)[1] - 1 + 127, 0) - down, 1)
    scale = np.exp2(byte - 127.0)
    codes = (blocks / scale).astype(np.float32).astype(dtype).astype(np.float64)
    return np.moveaxis((codes * scale).reshape(v.shape), -1, axis)


WIDE = False


def mx_kscale(k):
    if not WIDE:
        return np.ones(k)
    levels = np.array([10, -10, 5, -5, 0])
    if k % 512:
        return np.exp2(np.random.permutation(np.resize(levels, k // 32))).repeat(32)
    a = np.empty((k // 512, 16))
    for p in range(k // 512):
        a[p, :8] = np.random.permutation(np.resize(levels, 8))
        for g in range(8):
            far = levels[np.abs(levels - a[p, g]) >= 10]
            a[p, g + 8] = far[np.random.randint(len(far))]
    return np.exp2(a.ravel()).repeat(32)


def f64(x):
    return np.asarray(x).astype(np.float64)


def striped(idx):
    return np.tile(idx.reshape(-1, 16).T, (8, 1)).astype(np.uint16)


def unstriped(offs):
    return offs[:16].T.reshape(-1).astype(np.int64)


E2M1 = np.array([0.0, 0.5, 1.0, 1.5, 2.0, 3.0, 4.0, 6.0, -0.0, -0.5, -1.0, -1.5, -2.0, -3.0, -4.0, -6.0])


def pack_weight(w, fmt):
    k, n = w.shape
    w = f64(np.asarray(w, np.float32).astype(ml_dtypes.bfloat16)).reshape(k // 32, 32, n)
    amax = np.abs(w).max(1)
    if fmt == "e4m3":
        byte = np.frexp(amax)[1] - 1 + 127 - 7
    else:
        mant, ex = np.frexp(amax / 6.0)
        byte = np.where(mant > 0.5, ex, ex - 1) + 127
    byte = np.clip(np.where(amax > 0, byte, 1), 1, 254)
    scaled = (w * np.exp2(127.0 - byte)[:, None, :]).reshape(k, n).astype(np.float32)
    by_word = np.ascontiguousarray(scaled.reshape(k // 512, 128, 4, n).transpose(0, 1, 3, 2))
    if fmt == "e4m3":
        words = by_word.astype(ml_dtypes.float8_e4m3fn).view(np.uint8)
    else:
        c = by_word.astype(ml_dtypes.float4_e2m1fn).view(np.uint8) & 0xF
        words = (c[..., 0::2] | (c[..., 1::2] << 4)).reshape(k // 512, 128, 2 * n)
    return np.ascontiguousarray(words), np.ascontiguousarray(byte.astype(np.uint8).reshape(k // 512, 16, n))


def unpack_weight(words, scales, fmt):
    g, _, n = scales.shape
    words = np.ascontiguousarray(words).reshape(g, 128, n, -1)
    if fmt == "e4m3":
        vals = words.view(ml_dtypes.float8_e4m3fn).astype(np.float64)
    else:
        nib = np.empty((g, 128, n, 4), np.uint8)
        nib[..., 0::2] = words & 0xF
        nib[..., 1::2] = words >> 4
        vals = E2M1[nib]
    vals = vals * np.repeat(np.exp2(scales.astype(np.float64) - 127.0), 8, axis=1)[..., None]
    return vals.transpose(0, 1, 3, 2).reshape(g * 512, n)


def planes(y):
    n, m = y.shape
    v = y.astype(np.float32).astype(ml_dtypes.bfloat16).astype(np.float64).reshape(n // 32, 32, m)
    top = np.abs(v).max(1)
    byte = np.clip(np.where(top > 0, np.frexp(top)[1] - 1 + 127 - 7, 1), 1, 254)
    codes = (v * np.exp2(127.0 - byte)[:, None, :]).reshape(n, m).astype(np.float32).astype(ml_dtypes.float8_e4m3fn).view(np.uint8)
    words = codes.reshape(n // 512, 128, 4, m).transpose(0, 1, 3, 2)
    return np.ascontiguousarray(words), np.ascontiguousarray(byte.astype(np.uint8).reshape(n // 512, 16, m))


def silu(v):
    return v / (1.0 + np.exp(-np.maximum(v, -700.0)))


K, T, E, C, H, N = 1024, 512, 2, 256, 512, 512


def by_expert(wq, xq):
    return np.concatenate([wq[e].T @ xq[:, e * C:(e + 1) * C] for e in range(E)], axis=1)


def setup_inputs():
    n = np.random.standard_normal
    s = mx_kscale(K)
    u = mx_kscale(H)
    slot_token = np.random.permutation(T)[:E * C]
    x = pack_weight(n((K, T)) * s[:, None], "e4m3")
    wg = pack_weight(n((K, N)) / np.sqrt(K) / s[:, None], "e2m1")
    return {
        "x_words": x[0],
        "x_scales": x[1],
        "wg_words": wg[0],
        "wg_scales": wg[1],
        "w1": (n((E, K, H)) / np.sqrt(K) / s[None, :, None] * u).astype(np.float32),
        "w2": (n((E, H, N)) / np.sqrt(H) / u[None, :, None]).astype(np.float32),
        "gate": np.tile(np.random.uniform(0.2, 1.0, E * C), (128, 1)).astype(np.float32),
        "offs": striped(slot_token),
    }


def reference(x_words, x_scales, wg_words, wg_scales, w1, w2, gate, offs):
    wg = unpack_weight(wg_words, wg_scales, "e2m1")
    w1q = mxq(f64(w1), 1, "e4m3")
    w2q = mxq(f64(w2), 1, "e4m3")
    idx = unstriped(offs)
    x = unpack_weight(x_words, x_scales, "e4m3")
    o = silu(wg.T @ x)
    h = silu(by_expert(w1q, x[:, idx]))
    y = by_expert(w2q, mxq(h, 0, "e4m3"))
    c = np.zeros((N, T))
    c[:, idx] = f64(gate[:1]) * y
    out_0 = o * c
    return (out_0,) + planes(out_0)

@@ -1,0 +1,249 @@
+from contextlib import ExitStack
+
+import concourse.mybir as mybir
+from concourse.masks import make_identity
+
+K, T, E, C, H, N = 1024, 512, 2, 256, 512, 512
+FLOPS = 2 * K * N * T + 2 * K * H * E * C + 2 * H * N * E * C
+
+F32 = mybir.dt.float32
+BF16 = mybir.dt.bfloat16
+I32 = mybir.dt.int32
+U32 = mybir.dt.uint32
+U16 = mybir.dt.uint16
+U8 = mybir.dt.uint8
+FP8X4 = mybir.dt.float8_e4m3fn_x4
+FP4X4 = mybir.dt.float4_e2m1fn_x4
+SILU = mybir.ActivationFunctionType.Silu
+MULT = mybir.AluOpType.mult
+
+P = 128
+PACK = 4
+PASS = P * PACK
+PASSES = K // PASS
+QUADS = 4
+COLS = C // 16
+
+
+def tile_moe_ogt_silu_silu_kernel(
+    tc, x_words, x_scales, wg_words, wg_scales, w1, w2, gate, offs, out_0, out_1, out_2
+):
+    nc = tc.nc
+    with ExitStack() as ctx:
+        keep = ctx.enter_context(tc.tile_pool(name="keep", bufs=1))
+        ring = ctx.enter_context(tc.tile_pool(name="ring", bufs=4))
+        psum = ctx.enter_context(tc.psum_pool(name="psum", bufs=1))
+
+        def sb(name, shape, dtype):
+            return keep.tile(shape, dtype, name=name, tag=name, align_bytes=64)
+
+        offsets = keep.tile([P, E * COLS], U16, name="offsets")
+        xw = sb("xw", [P, PASSES, T], U32)
+        xs = sb("xs", [P, T], U8)
+        xs1 = sb("xs1", [P, T], U8)
+        wgw = sb("wgw", [P, PASSES, 2 * N], U8)
+        wgs = sb("wgs", [P, PASSES, N], U8)
+        gates = [sb("gate%d" % e, [P, C], F32) for e in range(E)]
+        ys = {}
+        ident = sb("ident", [P, P], F32)
+
+        mats = [(e, m) for e in range(E) for m in range(PASSES + 1)]
+        raw = {k: sb("raw%d%d" % k, [P, PACK, 512], F32) for k in mats}
+        grouped = {}
+        tags = {(1, 0, 0): "wq02", (1, 0, 1): "hq0"}
+        wq = {k: sb("wq%d%d" % k, [P, 512], U32) for k in mats}
+        wsc = {k: sb("wsc%d%d" % k, [P, 512], U8) for k in mats}
+        gw = {(e, s): sb("gw%d%d" % (e, s), [P, C], U32) for e in range(E) for s in range(PASSES)}
+        gs = [sb("gs%d" % e, [P, C], U8) for e in range(E)]
+        hq = [sb("hq%d" % e, [P, C], U32) for e in range(E)]
+        hs = [sb("hs%d" % e, [P, C], U8) for e in range(E)]
+        comb = {}
+        res = sb("res", [P, PACK, T], F32)
+        resb = sb("resb", [P, T, PACK], BF16)
+        rq = sb("rq", [P, T], U32)
+        rs = sb("rs", [P, T], U8)
+
+        def load_matrix(e, m):
+            rows = w1[e, m * PASS:(m + 1) * PASS, :] if m < PASSES else w2[e]
+            nc.sync.dma_start(out=raw[e, m][:], in_=rows.rearrange("(p j) c -> p j c", j=PACK))
+
+        def cast(key, half, on_vector):
+            ts = slice(2 * half, 2 * half + 2)
+            name = "grp%d%d%d" % (key + (half,))
+            grouped[key + (half,)] = keep.tile(
+                [P, 2, P, PACK], BF16, name=name, tag=tags.get(key + (half,), name), align_bytes=64
+            )
+            src = raw[key][:].rearrange("p j (m t) -> p m j t", t=PACK)[:, :, :, ts]
+            dst = grouped[key + (half,)][:].rearrange("p t m j -> p m j t")
+            if on_vector:
+                nc.vector.tensor_copy(out=dst, in_=src)
+            else:
+                nc.scalar.copy(out=dst, in_=src)
+
+        def quantise(key, half):
+            cols = slice(256 * half, 256 * half + 256)
+            nc.vector.quantize_mx(
+                out=wq[key][:, cols].bitcast(FP8X4),
+                scales=wsc[key][:, cols],
+                in_=grouped[key + (half,)][:].rearrange("p t m j -> p (t m j)"),
+            )
+
+        def gather(e):
+            lst = offsets[:, e * COLS:(e + 1) * COLS]
+            for s in range(PASSES):
+                nc.vector.tensor_copy(gw[e, s][:], xw[:, s, :].indirect(lst))
+            nc.vector.tensor_copy(gs[e][:], xs[:].indirect(lst))
+
+        def layer1(e):
+            banks = [psum.tile([P, PACK, P], F32, name="hbank", tag="wide", bufs=2) for c in range(2)]
+            for c in range(2):
+                slots = slice(c * P, (c + 1) * P)
+                for t in range(PACK):
+                    cols = slice(t * P, (t + 1) * P)
+                    for s in range(PASSES):
+                        nc.tensor.matmul_mx(
+                            out=banks[c][:, t, :],
+                            lhsT=wq[e, s][:, cols].bitcast(FP8X4),
+                            lhsT_scale=wsc[e, s][:, cols],
+                            rhs=gw[e, s][:, slots].bitcast(FP8X4),
+                            rhs_scale=gs[e][4 * s:P, slots],
+                            start=(s == 0),
+                            stop=(s == PASSES - 1),
+                        )
+            for c in range(2):
+                slots = slice(c * P, (c + 1) * P)
+                hb = sb("hb%d%d" % (e, c), [P, P, PACK], BF16)
+                nc.scalar.activation(out=hb[:], in_=banks[c][:].rearrange("p t n -> p n t"), func=SILU)
+                nc.vector.quantize_mx(
+                    out=hq[e][:, slots].bitcast(FP8X4),
+                    scales=hs[e][:, slots],
+                    in_=hb[:].rearrange("p n t -> p (n t)"),
+                )
+
+        def layer2(e, t, lo=0, hi=C):
+            cols = slice(t * P, (t + 1) * P)
+            bank = psum.tile([P, hi - lo], F32, name="ybank", bufs=2)
+            nc.tensor.matmul_mx(
+                out=bank[:],
+                lhsT=wq[e, PASSES][:, cols].bitcast(FP8X4),
+                lhsT_scale=wsc[e, PASSES][:, cols],
+                rhs=hq[e][:, lo:hi].bitcast(FP8X4),
+                rhs_scale=hs[e][:, lo:hi],
+                start=True,
+                stop=True,
+            )
+            ys[e, t, lo] = sb("y%d%d%d" % (e, t, lo), [P, hi - lo], F32)
+            nc.scalar.copy(out=ys[e, t, lo][:], in_=bank[:])
+
+        def scatter(e, t, lo=0, hi=C):
+            lst = offsets[:, (e * C + lo) // 16:(e * C + hi) // 16]
+            nc.vector.tensor_tensor(comb[t][:].indirect(lst), ys[e, t, lo][:], gates[e][:, lo:hi], MULT)
+
+        nc.vector.memset(xs[:].bitcast(I32), 0)
+        nc.gpsimd.memset(xs1[:].bitcast(I32), 0)
+        nc.gpsimd.memset(wgs[:].bitcast(I32), 0)
+        make_identity(nc, ident[:])
+        nc.sync.dma_start(offsets[:], offs)
+        nc.sync.dma_start(out=xw[:].bitcast(I32), in_=x_words.rearrange("s p t d -> p s (t d)").bitcast(I32))
+        for q in range(QUADS):
+            nc.sync.dma_start(
+                out=xs[32 * q:32 * q + 4 * PASSES, :].bitcast(I32), in_=x_scales[:, 4 * q:4 * q + 4, :].bitcast(I32)
+            )
+        for m in range(PASSES + 1):
+            load_matrix(0, m)
+        nc.sync.dma_start(out=gates[0][:], in_=gate[:, 0:C])
+        for m in range(PASSES + 1):
+            load_matrix(1, m)
+        nc.sync.dma_start(out=gates[1][:], in_=gate[:, C:2 * C])
+        nc.sync.dma_start(out=wgw[:].bitcast(I32), in_=wg_words.rearrange("s p c -> p s c").bitcast(I32))
+        for q in range(QUADS):
+            nc.sync.dma_start(
+                out=wgs[32 * q:32 * q + 4, :, :].bitcast(I32),
+                in_=wg_scales[:, 4 * q:4 * q + 4, :].rearrange("s r c -> r s c").bitcast(I32),
+            )
+            nc.sync.dma_start(
+                out=xs1[32 * q:32 * q + 4, :].bitcast(I32), in_=x_scales[1, 4 * q:4 * q + 4, :].bitcast(I32)
+            )
+
+        gather(0)
+        gather(1)
+        for m in range(PASSES):
+            cast((0, m), 0, True)
+            cast((0, m), 1, False)
+            quantise((0, m), 0)
+            quantise((0, m), 1)
+        layer1(0)
+        for half in range(2):
+            cast((0, PASSES), half, True)
+            quantise((0, PASSES), half)
+        layer2(0, 0, 0, P)
+        layer2(0, 0, P, C)
+        for t in range(1, PACK):
+            layer2(0, t)
+        for t in range(2):
+            comb[t] = sb("comb%d" % t, [P, T], F32)
+        scatter(0, 0, 0, P)
+        scatter(0, 0, P, C)
+        scatter(0, 1)
+
+        for m in range(PASSES):
+            for half in range(2):
+                cast((1, m), half, (m, half) == (1, 0))
+                quantise((1, m), half)
+        comb[2] = keep.tile([P, T], F32, name="comb2", tag="grp111", align_bytes=64)
+        scatter(0, 2)
+        cast((1, PASSES), 0, False)
+        quantise((1, PASSES), 0)
+        layer1(1)
+        comb[3] = keep.tile([P, T], F32, name="comb3", tag="hb11", align_bytes=64)
+        scatter(0, 3)
+        cast((1, PASSES), 1, False)
+        quantise((1, PASSES), 1)
+        for t in range(PACK):
+            layer2(1, t)
+            scatter(1, t)
+
+        obanks = [psum.tile([P, T], F32, name="obank%d" % t) for t in range(PACK)]
+        for c in range(T // P):
+            toks = slice(c * P, (c + 1) * P)
+            bank = psum.tile([P, N], F32, name="gbank", tag="wide", bufs=2)
+            for s in range(PASSES):
+                nc.tensor.matmul_mx(
+                    out=bank[:],
+                    lhsT=xw[:, s, toks].bitcast(FP8X4),
+                    lhsT_scale=(xs if s == 0 else xs1)[:, toks],
+                    rhs=wgw[:, s, :].bitcast(FP4X4),
+                    rhs_scale=wgs[:, s, :],
+                    start=(s == 0),
+                    stop=(s == PASSES - 1),
+                )
+            ot = ring.tile([P, PACK, P], F32, name="ot")
+            nc.scalar.activation(out=ot[:], in_=bank[:].rearrange("p (m t) -> p t m", t=PACK), func=SILU)
+            for t in range(PACK):
+                nc.tensor.transpose(obanks[t][:, toks], ot[:, t, :], ident[:])
+
+        out_rows = out_0.rearrange("(p t) c -> p t c", t=PACK)
+        for t in range(PACK):
+            nc.vector.tensor_tensor(res[:, t, :], obanks[t][:], comb[t][:], MULT)
+            nc.sync.dma_start(out=out_rows[:, t, :], in_=res[:, t, :])
+
+        words = out_1[0].rearrange("p c d -> p (c d)").bitcast(I32)
+        for half in (1, 0):
+            toks = slice(half * 256, half * 256 + 256)
+            src = res[:, :, toks].rearrange("p t (c i) -> p c t i", i=4)
+            dst = resb[:, toks, :].rearrange("p (c i) t -> p c t i", i=4)
+            if half == 1:
+                nc.vector.tensor_copy(out=dst, in_=src)
+            else:
+                nc.scalar.copy(out=dst, in_=src)
+            nc.vector.quantize_mx(
+                out=rq[:, toks].bitcast(FP8X4),
+                scales=rs[:, toks],
+                in_=resb[:, toks, :].rearrange("p c t -> p (c t)"),
+            )
+            nc.sync.dma_start(out=words[:, toks], in_=rq[:, toks].bitcast(I32))
+        for q in range(QUADS):
+            queue = nc.sync if q % 2 == 0 else nc.scalar
+            queue.dma_start(
+                out=out_2[0, 4 * q:4 * q + 4, :].bitcast(I32), in_=rs[32 * q:32 * q + 4, :].bitcast(I32)
+            )

@@ -32,9 +32,23 @@ def tile_moe_ogt_silu_silu_kernel(
     with ExitStack() as ctx:
         keep = ctx.enter_context(tc.tile_pool(name="keep", bufs=1))
         ring = ctx.enter_context(tc.tile_pool(name="ring", bufs=4))
+        lap = ctx.enter_context(tc.tile_pool(name="lap", bufs=1))
         psum = ctx.enter_context(tc.psum_pool(name="psum", bufs=1))
 
+        places = {
+            "grp011": 0, "grp020": 0,
+            "hb00": 2048, "grp021": 2048,
+            "wq020": 4096, "grp10": 4096, "grp111": 6144, "comb2": 7168,
+            "hq0": 8192, "grp110": 8192,
+            "wsc021": 16384, "grp12": 16384,
+            "y010": 20480, "wsc10": 20480,
+            "hb10": 21504, "comb3": 21504,
+            "raw10": 24576, "y020": 24576, "y030": 25600, "wsc12": 24576,
+        }
+
         def sb(name, shape, dtype):
+            if name in places:
+                return lap.tile(shape, dtype, name=name, tag=name, align_bytes=64, offset=places[name])
             return keep.tile(shape, dtype, name=name, tag=name, align_bytes=64)
 
         offsets = keep.tile([P, E * COLS], U16, name="offsets")
@@ -50,11 +64,10 @@ def tile_moe_ogt_silu_silu_kernel(
         mats = [(e, m) for e in range(E) for m in range(PASSES + 1)]
         raw = {k: sb("raw%d%d" % k, [P, PACK, 512], F32) for k in mats}
         grouped = {}
-        tags = {(1, 0, 0): "wq02", (1, 0, 1): "hq0"}
-        wq = {k: sb("wq%d%d" % k, [P, 512], U32) for k in mats}
-        wsc = {k: sb("wsc%d%d" % k, [P, 512], U8) for k in mats}
+        wq = {}
+        wsc = {}
         gw = {(e, s): sb("gw%d%d" % (e, s), [P, C], U32) for e in range(E) for s in range(PASSES)}
-        gs = [sb("gs%d" % e, [P, C], U8) for e in range(E)]
+        gs = {}
         hq = [sb("hq%d" % e, [P, C], U32) for e in range(E)]
         hs = [sb("hs%d" % e, [P, C], U8) for e in range(E)]
         comb = {}
@@ -67,44 +80,51 @@ def tile_moe_ogt_silu_silu_kernel(
             rows = w1[e, m * PASS:(m + 1) * PASS, :] if m < PASSES else w2[e]
             nc.sync.dma_start(out=raw[e, m][:], in_=rows.rearrange("(p j) c -> p j c", j=PACK))
 
-        def cast(key, half, on_vector):
-            ts = slice(2 * half, 2 * half + 2)
-            name = "grp%d%d%d" % (key + (half,))
-            grouped[key + (half,)] = keep.tile(
-                [P, 2, P, PACK], BF16, name=name, tag=tags.get(key + (half,), name), align_bytes=64
-            )
-            src = raw[key][:].rearrange("p j (m t) -> p m j t", t=PACK)[:, :, :, ts]
-            dst = grouped[key + (half,)][:].rearrange("p t m j -> p m j t")
+        def label(key, lo, hi):
+            return "%d%d" % key if hi - lo == PACK else "%d%d%d" % (key + (lo // 2,))
+
+        def cast(key, lo, hi, on_vector):
+            name = label(key, lo, hi)
+            grouped[name] = sb("grp" + name, [P, hi - lo, P, PACK], BF16)
+            src = raw[key][:].rearrange("p j (m t) -> p m j t", t=PACK)[:, :, :, lo:hi]
+            dst = grouped[name][:].rearrange("p t m j -> p m j t")
             if on_vector:
                 nc.vector.tensor_copy(out=dst, in_=src)
             else:
                 nc.scalar.copy(out=dst, in_=src)
 
-        def quantise(key, half):
-            cols = slice(256 * half, 256 * half + 256)
+        def quantise(key, lo, hi):
+            name = label(key, lo, hi)
+            codes = sb("wq" + name, [P, (hi - lo) * P], U32)
+            scales = sb("wsc" + name, [P, (hi - lo) * P], U8)
             nc.vector.quantize_mx(
-                out=wq[key][:, cols].bitcast(FP8X4),
-                scales=wsc[key][:, cols],
-                in_=grouped[key + (half,)][:].rearrange("p t m j -> p (t m j)"),
+                out=codes[:].bitcast(FP8X4),
+                scales=scales[:],
+                in_=grouped[name][:].rearrange("p t m j -> p (t m j)"),
             )
+            for t in range(lo, hi):
+                cols = slice((t - lo) * P, (t - lo + 1) * P)
+                wq[key + (t,)] = codes[:, cols].bitcast(FP8X4)
+                wsc[key + (t,)] = scales[:, cols]
 
-        def gather(e):
-            lst = offsets[:, e * COLS:(e + 1) * COLS]
+        def gather_words(e):
             for s in range(PASSES):
-                nc.vector.tensor_copy(gw[e, s][:], xw[:, s, :].indirect(lst))
-            nc.vector.tensor_copy(gs[e][:], xs[:].indirect(lst))
+                nc.vector.tensor_copy(gw[e, s][:], xw[:, s, :].indirect(offsets[:, e * COLS:(e + 1) * COLS]))
+
+        def gather_scales(e):
+            gs[e] = sb("gs%d" % e, [P, C], U8)
+            nc.vector.tensor_copy(gs[e][:], xs[:].indirect(offsets[:, e * COLS:(e + 1) * COLS]))
 
         def layer1(e):
-            banks = [psum.tile([P, PACK, P], F32, name="hbank", tag="wide", bufs=2) for c in range(2)]
+            banks = [psum.tile([P, PACK, P], F32, name="hbank", tag="bank%d" % c) for c in range(2)]
             for c in range(2):
                 slots = slice(c * P, (c + 1) * P)
                 for t in range(PACK):
-                    cols = slice(t * P, (t + 1) * P)
                     for s in range(PASSES):
                         nc.tensor.matmul_mx(
                             out=banks[c][:, t, :],
-                            lhsT=wq[e, s][:, cols].bitcast(FP8X4),
-                            lhsT_scale=wsc[e, s][:, cols],
+                            lhsT=wq[e, s, t],
+                            lhsT_scale=wsc[e, s, t],
                             rhs=gw[e, s][:, slots].bitcast(FP8X4),
                             rhs_scale=gs[e][4 * s:P, slots],
                             start=(s == 0),
@@ -113,20 +133,23 @@ def tile_moe_ogt_silu_silu_kernel(
             for c in range(2):
                 slots = slice(c * P, (c + 1) * P)
                 hb = sb("hb%d%d" % (e, c), [P, P, PACK], BF16)
-                nc.scalar.activation(out=hb[:], in_=banks[c][:].rearrange("p t n -> p n t"), func=SILU)
+                nc.scalar.activation(
+                    out=hb[:].rearrange("p (c i) t -> p c t i", i=2),
+                    in_=banks[c][:].rearrange("p t (c i) -> p c t i", i=2),
+                    func=SILU,
+                )
                 nc.vector.quantize_mx(
                     out=hq[e][:, slots].bitcast(FP8X4),
                     scales=hs[e][:, slots],
                     in_=hb[:].rearrange("p n t -> p (n t)"),
                 )
 
-        def layer2(e, t, lo=0, hi=C):
-            cols = slice(t * P, (t + 1) * P)
-            bank = psum.tile([P, hi - lo], F32, name="ybank", bufs=2)
+        def layer2(e, t, where, lo=0, hi=C):
+            bank = psum.tile([P, hi - lo], F32, name="ybank", tag="bank%d" % where)
             nc.tensor.matmul_mx(
                 out=bank[:],
-                lhsT=wq[e, PASSES][:, cols].bitcast(FP8X4),
-                lhsT_scale=wsc[e, PASSES][:, cols],
+                lhsT=wq[e, PASSES, t],
+                lhsT_scale=wsc[e, PASSES, t],
                 rhs=hq[e][:, lo:hi].bitcast(FP8X4),
                 rhs_scale=hs[e][:, lo:hi],
                 start=True,
@@ -139,6 +162,9 @@ def tile_moe_ogt_silu_silu_kernel(
             lst = offsets[:, (e * C + lo) // 16:(e * C + hi) // 16]
             nc.vector.tensor_tensor(comb[t][:].indirect(lst), ys[e, t, lo][:], gates[e][:, lo:hi], MULT)
 
+        warm = sb("warm", [P, 2], F32)
+        nc.vector.memset(warm[:, 0:1], 0.0)
+        nc.scalar.activation(out=warm[:, 1:2], in_=warm[:, 0:1], func=SILU)
         nc.vector.memset(xs[:].bitcast(I32), 0)
         nc.gpsimd.memset(xs1[:].bitcast(I32), 0)
         nc.gpsimd.memset(wgs[:].bitcast(I32), 0)
@@ -165,48 +191,59 @@ def tile_moe_ogt_silu_silu_kernel(
                 out=xs1[32 * q:32 * q + 4, :].bitcast(I32), in_=x_scales[1, 4 * q:4 * q + 4, :].bitcast(I32)
             )
 
-        gather(0)
-        gather(1)
-        for m in range(PASSES):
-            cast((0, m), 0, True)
-            cast((0, m), 1, False)
-            quantise((0, m), 0)
-            quantise((0, m), 1)
+        gather_words(0)
+        gather_scales(0)
+        gather_words(1)
+        gather_scales(1)
+        cast((0, 0), 0, 2, False)
+        quantise((0, 0), 0, 2)
+        cast((0, 0), 2, 4, False)
+        cast((0, 1), 0, 2, True)
+        cast((0, 1), 2, 4, False)
+        quantise((0, 0), 2, 4)
+        quantise((0, 1), 0, 2)
+        quantise((0, 1), 2, 4)
+        cast((0, 2), 0, 2, True)
+        quantise((0, 2), 0, 2)
         layer1(0)
-        for half in range(2):
-            cast((0, PASSES), half, True)
-            quantise((0, PASSES), half)
-        layer2(0, 0, 0, P)
-        layer2(0, 0, P, C)
-        for t in range(1, PACK):
-            layer2(0, t)
-        for t in range(2):
-            comb[t] = sb("comb%d" % t, [P, T], F32)
+        layer2(0, 0, 2, 0, P)
+        cast((0, 2), 2, 4, True)
+        layer2(0, 0, 3, P, C)
+        comb[0] = sb("comb0", [P, T], F32)
         scatter(0, 0, 0, P)
+        quantise((0, 2), 2, 4)
         scatter(0, 0, P, C)
+        layer2(0, 1, 0)
+        comb[1] = sb("comb1", [P, T], F32)
         scatter(0, 1)
 
-        for m in range(PASSES):
-            for half in range(2):
-                cast((1, m), half, (m, half) == (1, 0))
-                quantise((1, m), half)
-        comb[2] = keep.tile([P, T], F32, name="comb2", tag="grp111", align_bytes=64)
+        cast((1, 0), 0, 4, False)
+        layer2(0, 2, 1)
+        layer2(0, 3, 2)
+        quantise((1, 0), 0, 4)
+        cast((1, 1), 0, 2, False)
+        cast((1, 1), 2, 4, True)
+        quantise((1, 1), 0, 2)
+        quantise((1, 1), 2, 4)
+        comb[2] = sb("comb2", [P, T], F32)
         scatter(0, 2)
-        cast((1, PASSES), 0, False)
-        quantise((1, PASSES), 0)
+        cast((1, 2), 0, 4, False)
+        quantise((1, 2), 0, 4)
         layer1(1)
-        comb[3] = keep.tile([P, T], F32, name="comb3", tag="hb11", align_bytes=64)
+        comb[3] = sb("comb3", [P, T], F32)
         scatter(0, 3)
-        cast((1, PASSES), 1, False)
-        quantise((1, PASSES), 1)
-        for t in range(PACK):
-            layer2(1, t)
+        layer2(1, 0, 2, 0, P)
+        scatter(1, 0, 0, P)
+        layer2(1, 0, 3, P, C)
+        scatter(1, 0, P, C)
+        for t in range(1, PACK):
+            layer2(1, t, t - 1)
             scatter(1, t)
 
         obanks = [psum.tile([P, T], F32, name="obank%d" % t) for t in range(PACK)]
         for c in range(T // P):
             toks = slice(c * P, (c + 1) * P)
-            bank = psum.tile([P, N], F32, name="gbank", tag="wide", bufs=2)
+            bank = psum.tile([P, N], F32, name="gbank", tag="bank%d" % ((c + 3) % 4))
             for s in range(PASSES):
                 nc.tensor.matmul_mx(
                     out=bank[:],
@@ -218,7 +255,11 @@ def tile_moe_ogt_silu_silu_kernel(
                     stop=(s == PASSES - 1),
                 )
             ot = ring.tile([P, PACK, P], F32, name="ot")
-            nc.scalar.activation(out=ot[:], in_=bank[:].rearrange("p (m t) -> p t m", t=PACK), func=SILU)
+            nc.scalar.activation(
+                out=ot[:].rearrange("p (h l) m -> p h m l", l=2),
+                in_=bank[:].rearrange("p (m h l) -> p h m l", h=2, l=2),
+                func=SILU,
+            )
             for t in range(PACK):
                 nc.tensor.transpose(obanks[t][:, toks], ot[:, t, :], ident[:])
 

@@ -31,19 +31,17 @@ def tile_moe_ogt_silu_silu_kernel(
     nc = tc.nc
     with ExitStack() as ctx:
         keep = ctx.enter_context(tc.tile_pool(name="keep", bufs=1))
-        ring = ctx.enter_context(tc.tile_pool(name="ring", bufs=4))
         lap = ctx.enter_context(tc.tile_pool(name="lap", bufs=1))
         psum = ctx.enter_context(tc.psum_pool(name="psum", bufs=1))
 
         places = {
-            "grp011": 0, "grp020": 0,
-            "hb00": 2048, "grp021": 2048,
-            "wq020": 4096, "grp10": 4096, "grp111": 6144, "comb2": 7168,
-            "hq0": 8192, "grp110": 8192,
-            "wsc021": 16384, "grp12": 16384,
-            "y010": 20480, "wsc10": 20480,
-            "hb10": 21504, "comb3": 21504,
-            "raw10": 24576, "y020": 24576, "y030": 25600, "wsc12": 24576,
+            "grp011": 0, "gw11": 0, "grp02": 1024,
+            "wq020": 5120, "grp10": 5120,
+            "raw02": 43008, "hq0": 43008, "grp110": 43008, "grp12": 43008,
+            "raw10": 16384, "grp111": 18432,
+            "raw11": 24576, "comb2": 24576, "y020": 26624, "y030": 27648,
+            "raw12": 32768, "y03128": 34816,
+            "hb11": 40960, "ot0": 40960,
         }
 
         def sb(name, shape, dtype):
@@ -52,7 +50,7 @@ def tile_moe_ogt_silu_silu_kernel(
             return keep.tile(shape, dtype, name=name, tag=name, align_bytes=64)
 
         offsets = keep.tile([P, E * COLS], U16, name="offsets")
-        xw = sb("xw", [P, PASSES, T], U32)
+        xw = [sb("xw%d" % s, [P, T], U32) for s in range(PASSES)]
         xs = sb("xs", [P, T], U8)
         xs1 = sb("xs1", [P, T], U8)
         wgw = sb("wgw", [P, PASSES, 2 * N], U8)
@@ -66,9 +64,9 @@ def tile_moe_ogt_silu_silu_kernel(
         grouped = {}
         wq = {}
         wsc = {}
-        gw = {(e, s): sb("gw%d%d" % (e, s), [P, C], U32) for e in range(E) for s in range(PASSES)}
+        gw = {}
         gs = {}
-        hq = [sb("hq%d" % e, [P, C], U32) for e in range(E)]
+        hq = {}
         hs = [sb("hs%d" % e, [P, C], U8) for e in range(E)]
         comb = {}
         res = sb("res", [P, PACK, T], F32)
@@ -95,21 +93,25 @@ def tile_moe_ogt_silu_silu_kernel(
 
         def quantise(key, lo, hi):
             name = label(key, lo, hi)
+            source = grouped[name][:] if name in grouped else grouped["%d%d" % key][:, lo:hi, :, :]
             codes = sb("wq" + name, [P, (hi - lo) * P], U32)
             scales = sb("wsc" + name, [P, (hi - lo) * P], U8)
             nc.vector.quantize_mx(
                 out=codes[:].bitcast(FP8X4),
                 scales=scales[:],
-                in_=grouped[name][:].rearrange("p t m j -> p (t m j)"),
+                in_=source.rearrange("p t m j -> p (t m j)"),
             )
             for t in range(lo, hi):
                 cols = slice((t - lo) * P, (t - lo + 1) * P)
                 wq[key + (t,)] = codes[:, cols].bitcast(FP8X4)
                 wsc[key + (t,)] = scales[:, cols]
 
-        def gather_words(e):
-            for s in range(PASSES):
-                nc.vector.tensor_copy(gw[e, s][:], xw[:, s, :].indirect(offsets[:, e * COLS:(e + 1) * COLS]))
+        def load_words(s):
+            nc.sync.dma_start(out=xw[s][:].bitcast(I32), in_=x_words[s].rearrange("p t d -> p (t d)").bitcast(I32))
+
+        def gather_words(e, s):
+            gw[e, s] = sb("gw%d%d" % (e, s), [P, C], U32)
+            nc.vector.tensor_copy(gw[e, s][:], xw[s][:].indirect(offsets[:, e * COLS:(e + 1) * COLS]))
 
         def gather_scales(e):
             gs[e] = sb("gs%d" % e, [P, C], U8)
@@ -130,19 +132,23 @@ def tile_moe_ogt_silu_silu_kernel(
                             start=(s == 0),
                             stop=(s == PASSES - 1),
                         )
-            for c in range(2):
-                slots = slice(c * P, (c + 1) * P)
-                hb = sb("hb%d%d" % (e, c), [P, P, PACK], BF16)
-                nc.scalar.activation(
-                    out=hb[:].rearrange("p (c i) t -> p c t i", i=2),
-                    in_=banks[c][:].rearrange("p t (c i) -> p c t i", i=2),
-                    func=SILU,
-                )
-                nc.vector.quantize_mx(
-                    out=hq[e][:, slots].bitcast(FP8X4),
-                    scales=hs[e][:, slots],
-                    in_=hb[:].rearrange("p n t -> p (n t)"),
-                )
+            return banks
+
+        def hidden(e, c, banks):
+            slots = slice(c * P, (c + 1) * P)
+            hb = sb("hb%d%d" % (e, c), [P, P, PACK], BF16)
+            if c == 0:
+                hq[e] = sb("hq%d" % e, [P, C], U32)
+            nc.scalar.activation(
+                out=hb[:].rearrange("p (c i) t -> p c t i", i=2),
+                in_=banks[c][:].rearrange("p t (c i) -> p c t i", i=2),
+                func=SILU,
+            )
+            nc.vector.quantize_mx(
+                out=hq[e][:, slots].bitcast(FP8X4),
+                scales=hs[e][:, slots],
+                in_=hb[:].rearrange("p n t -> p (n t)"),
+            )
 
         def layer2(e, t, where, lo=0, hi=C):
             bank = psum.tile([P, hi - lo], F32, name="ybank", tag="bank%d" % where)
@@ -155,28 +161,33 @@ def tile_moe_ogt_silu_silu_kernel(
                 start=True,
                 stop=True,
             )
+            return bank
+
+        def copy_out(e, t, bank, lo=0, hi=C):
             ys[e, t, lo] = sb("y%d%d%d" % (e, t, lo), [P, hi - lo], F32)
-            nc.scalar.copy(out=ys[e, t, lo][:], in_=bank[:])
+            nc.scalar.copy(out=ys[e, t, lo][:], in_=bank)
+
+        def rows(e, t, where, lo=0, hi=C):
+            copy_out(e, t, layer2(e, t, where, lo, hi)[:], lo, hi)
 
         def scatter(e, t, lo=0, hi=C):
             lst = offsets[:, (e * C + lo) // 16:(e * C + hi) // 16]
             nc.vector.tensor_tensor(comb[t][:].indirect(lst), ys[e, t, lo][:], gates[e][:, lo:hi], MULT)
 
-        warm = sb("warm", [P, 2], F32)
-        nc.vector.memset(warm[:, 0:1], 0.0)
-        nc.scalar.activation(out=warm[:, 1:2], in_=warm[:, 0:1], func=SILU)
         nc.vector.memset(xs[:].bitcast(I32), 0)
         nc.gpsimd.memset(xs1[:].bitcast(I32), 0)
         nc.gpsimd.memset(wgs[:].bitcast(I32), 0)
         make_identity(nc, ident[:])
         nc.sync.dma_start(offsets[:], offs)
-        nc.sync.dma_start(out=xw[:].bitcast(I32), in_=x_words.rearrange("s p t d -> p s (t d)").bitcast(I32))
+        load_words(0)
         for q in range(QUADS):
             nc.sync.dma_start(
                 out=xs[32 * q:32 * q + 4 * PASSES, :].bitcast(I32), in_=x_scales[:, 4 * q:4 * q + 4, :].bitcast(I32)
             )
-        for m in range(PASSES + 1):
-            load_matrix(0, m)
+        load_matrix(0, 0)
+        load_matrix(0, 1)
+        load_words(1)
+        load_matrix(0, 2)
         nc.sync.dma_start(out=gates[0][:], in_=gate[:, 0:C])
         for m in range(PASSES + 1):
             load_matrix(1, m)
@@ -191,70 +202,77 @@ def tile_moe_ogt_silu_silu_kernel(
                 out=xs1[32 * q:32 * q + 4, :].bitcast(I32), in_=x_scales[1, 4 * q:4 * q + 4, :].bitcast(I32)
             )
 
-        gather_words(0)
+        gather_words(0, 0)
         gather_scales(0)
-        gather_words(1)
+        gather_words(1, 0)
         gather_scales(1)
-        cast((0, 0), 0, 2, False)
-        quantise((0, 0), 0, 2)
+        cast((0, 0), 0, 2, True)
         cast((0, 0), 2, 4, False)
+        quantise((0, 0), 0, 2)
+        quantise((0, 0), 2, 4)
         cast((0, 1), 0, 2, True)
         cast((0, 1), 2, 4, False)
-        quantise((0, 0), 2, 4)
+        gather_words(0, 1)
         quantise((0, 1), 0, 2)
         quantise((0, 1), 2, 4)
-        cast((0, 2), 0, 2, True)
+        gather_words(1, 1)
+        cast((0, 2), 0, 4, True)
         quantise((0, 2), 0, 2)
-        layer1(0)
-        layer2(0, 0, 2, 0, P)
-        cast((0, 2), 2, 4, True)
-        layer2(0, 0, 3, P, C)
-        comb[0] = sb("comb0", [P, T], F32)
-        scatter(0, 0, 0, P)
+        banks = layer1(0)
+        hidden(0, 0, banks)
         quantise((0, 2), 2, 4)
-        scatter(0, 0, P, C)
-        layer2(0, 1, 0)
-        comb[1] = sb("comb1", [P, T], F32)
-        scatter(0, 1)
+        hidden(0, 1, banks)
+        for t in range(2):
+            comb[t] = sb("comb%d" % t, [P, T], F32)
+        for c in range(2):
+            for t in range(2):
+                rows(0, t, 2 + 2 * c + t, c * P, (c + 1) * P)
+                scatter(0, t, c * P, (c + 1) * P)
 
         cast((1, 0), 0, 4, False)
-        layer2(0, 2, 1)
-        layer2(0, 3, 2)
+        second = layer2(0, 2, 1)
+        last = layer2(0, 3, 2)
         quantise((1, 0), 0, 4)
         cast((1, 1), 0, 2, False)
         cast((1, 1), 2, 4, True)
         quantise((1, 1), 0, 2)
         quantise((1, 1), 2, 4)
-        comb[2] = sb("comb2", [P, T], F32)
+        copy_out(0, 2, second[:])
+        copy_out(0, 3, last[:, 0:P], 0, P)
+        for t in range(2, PACK):
+            comb[t] = sb("comb%d" % t, [P, T], F32)
         scatter(0, 2)
+        scatter(0, 3, 0, P)
         cast((1, 2), 0, 4, False)
         quantise((1, 2), 0, 4)
-        layer1(1)
-        comb[3] = sb("comb3", [P, T], F32)
-        scatter(0, 3)
-        layer2(1, 0, 2, 0, P)
-        scatter(1, 0, 0, P)
-        layer2(1, 0, 3, P, C)
-        scatter(1, 0, P, C)
-        for t in range(1, PACK):
-            layer2(1, t, t - 1)
+        banks = layer1(1)
+        hidden(1, 0, banks)
+        copy_out(0, 3, last[:, P:C], P, C)
+        scatter(0, 3, P, C)
+        hidden(1, 1, banks)
+        for c in range(2):
+            for t in range(2):
+                rows(1, t, 2 + 2 * c + t, c * P, (c + 1) * P)
+                scatter(1, t, c * P, (c + 1) * P)
+        for t in range(2, PACK):
+            rows(1, t, 4 + t)
             scatter(1, t)
 
-        obanks = [psum.tile([P, T], F32, name="obank%d" % t) for t in range(PACK)]
+        obanks = [psum.tile([P, T], F32, name="obank%d" % t, tag="bank%d" % (4 + t)) for t in range(PACK)]
         for c in range(T // P):
             toks = slice(c * P, (c + 1) * P)
-            bank = psum.tile([P, N], F32, name="gbank", tag="bank%d" % ((c + 3) % 4))
+            bank = psum.tile([P, N], F32, name="gbank", tag="bank%d" % c)
             for s in range(PASSES):
                 nc.tensor.matmul_mx(
                     out=bank[:],
-                    lhsT=xw[:, s, toks].bitcast(FP8X4),
+                    lhsT=xw[s][:, toks].bitcast(FP8X4),
                     lhsT_scale=(xs if s == 0 else xs1)[:, toks],
                     rhs=wgw[:, s, :].bitcast(FP4X4),
                     rhs_scale=wgs[:, s, :],
                     start=(s == 0),
                     stop=(s == PASSES - 1),
                 )
-            ot = ring.tile([P, PACK, P], F32, name="ot")
+            ot = sb("ot%d" % c, [P, PACK, P], F32)
             nc.scalar.activation(
                 out=ot[:].rearrange("p (h l) m -> p h m l", l=2),
                 in_=bank[:].rearrange("p (m h l) -> p h m l", h=2, l=2),
@@ -264,19 +282,20 @@ def tile_moe_ogt_silu_silu_kernel(
                 nc.tensor.transpose(obanks[t][:, toks], ot[:, t, :], ident[:])
 
         out_rows = out_0.rearrange("(p t) c -> p t c", t=PACK)
-        for t in range(PACK):
-            nc.vector.tensor_tensor(res[:, t, :], obanks[t][:], comb[t][:], MULT)
-            nc.sync.dma_start(out=out_rows[:, t, :], in_=res[:, t, :])
+        for half in range(2):
+            toks = slice(half * 256, half * 256 + 256)
+            for t in range(PACK):
+                nc.vector.tensor_tensor(res[:, t, toks], obanks[t][:, toks], comb[t][:, toks], MULT)
+            nc.sync.dma_start(out=out_rows[:, :, toks], in_=res[:, :, toks])
 
         words = out_1[0].rearrange("p c d -> p (c d)").bitcast(I32)
-        for half in (1, 0):
-            toks = slice(half * 256, half * 256 + 256)
-            src = res[:, :, toks].rearrange("p t (c i) -> p c t i", i=4)
-            dst = resb[:, toks, :].rearrange("p (c i) t -> p c t i", i=4)
-            if half == 1:
-                nc.vector.tensor_copy(out=dst, in_=src)
-            else:
-                nc.scalar.copy(out=dst, in_=src)
+        halves = [slice(half * 256, half * 256 + 256) for half in range(2)]
+        for toks, copy in zip(halves, (nc.scalar.copy, nc.vector.tensor_copy)):
+            copy(
+                out=resb[:, toks, :].rearrange("p (c i) t -> p c t i", i=4),
+                in_=res[:, :, toks].rearrange("p t (c i) -> p c t i", i=4),
+            )
+        for toks in halves:
             nc.vector.quantize_mx(
                 out=rq[:, toks].bitcast(FP8X4),
                 scales=rs[:, toks],

@@ -21,8 +21,37 @@ P = 128
 PACK = 4
 PASS = P * PACK
 PASSES = K // PASS
-QUADS = 4
-COLS = C // 16
+SECOND = PASSES
+WIDTH = 512
+PAIR = PACK // 2
+QUADRANT = 32
+SCALE_ROWS = 4
+PER_COLUMN = 16
+CHUNKS = C // P
+HALF = T // 2
+KIB = 1024
+
+SHARED = {
+    "grp011": 0,
+    "gw11": 0,
+    "grp02": 1 * KIB,
+    "wq020": 5 * KIB,
+    "grp10": 5 * KIB,
+    "raw10": 16 * KIB,
+    "grp111": 18 * KIB,
+    "raw11": 24 * KIB,
+    "comb2": 24 * KIB,
+    "y020": 26 * KIB,
+    "y030": 27 * KIB,
+    "raw12": 32 * KIB,
+    "y03128": 34 * KIB,
+    "hb11": 40 * KIB,
+    "ot0": 40 * KIB,
+    "raw02": 42 * KIB,
+    "hq0": 42 * KIB,
+    "grp110": 42 * KIB,
+    "grp12": 42 * KIB,
+}
 
 
 def tile_moe_ogt_silu_silu_kernel(
@@ -31,71 +60,66 @@ def tile_moe_ogt_silu_silu_kernel(
     nc = tc.nc
     with ExitStack() as ctx:
         keep = ctx.enter_context(tc.tile_pool(name="keep", bufs=1))
-        lap = ctx.enter_context(tc.tile_pool(name="lap", bufs=1))
+        shared = ctx.enter_context(tc.tile_pool(name="lap", bufs=1))
         psum = ctx.enter_context(tc.psum_pool(name="psum", bufs=1))
 
-        places = {
-            "grp011": 0, "gw11": 0, "grp02": 1024,
-            "wq020": 5120, "grp10": 5120,
-            "raw02": 43008, "hq0": 43008, "grp110": 43008, "grp12": 43008,
-            "raw10": 16384, "grp111": 18432,
-            "raw11": 24576, "comb2": 24576, "y020": 26624, "y030": 27648,
-            "raw12": 32768, "y03128": 34816,
-            "hb11": 40960, "ot0": 40960,
-        }
-
-        def sb(name, shape, dtype):
-            if name in places:
-                return lap.tile(shape, dtype, name=name, tag=name, align_bytes=64, offset=places[name])
+        def sbuf(name, shape, dtype):
+            if name in SHARED:
+                return shared.tile(shape, dtype, name=name, tag=name, align_bytes=64, offset=SHARED[name])
             return keep.tile(shape, dtype, name=name, tag=name, align_bytes=64)
 
-        offsets = keep.tile([P, E * COLS], U16, name="offsets")
-        xw = [sb("xw%d" % s, [P, T], U32) for s in range(PASSES)]
-        xs = sb("xs", [P, T], U8)
-        xs1 = sb("xs1", [P, T], U8)
-        wgw = sb("wgw", [P, PASSES, 2 * N], U8)
-        wgs = sb("wgs", [P, PASSES, N], U8)
-        gates = [sb("gate%d" % e, [P, C], F32) for e in range(E)]
-        ys = {}
-        ident = sb("ident", [P, P], F32)
+        def bank_tile(name, shape, bank):
+            return psum.tile(shape, F32, name=name, tag="bank%d" % bank)
 
-        mats = [(e, m) for e in range(E) for m in range(PASSES + 1)]
-        raw = {k: sb("raw%d%d" % k, [P, PACK, 512], F32) for k in mats}
-        grouped = {}
-        wq = {}
-        wsc = {}
-        gw = {}
-        gs = {}
-        hq = {}
-        hs = [sb("hs%d" % e, [P, C], U8) for e in range(E)]
-        comb = {}
-        res = sb("res", [P, PACK, T], F32)
-        resb = sb("resb", [P, T, PACK], BF16)
-        rq = sb("rq", [P, T], U32)
-        rs = sb("rs", [P, T], U8)
+        offsets = keep.tile([P, E * C // PER_COLUMN], U16, name="offsets")
+        token_words = [sbuf("xw%d" % s, [P, T], U32) for s in range(PASSES)]
+        token_scales = sbuf("xs", [P, T], U8)
+        second_pass_scales = sbuf("xs1", [P, T], U8)
+        gate_words = sbuf("wgw", [P, PASSES, 2 * N], U8)
+        gate_scales = sbuf("wgs", [P, PASSES, N], U8)
+        slot_weights = [sbuf("gate%d" % e, [P, C], F32) for e in range(E)]
+        identity = sbuf("ident", [P, P], F32)
+        matrices = [(e, m) for e in range(E) for m in range(PASSES + 1)]
+        loaded = {matrix: sbuf("raw%d%d" % matrix, [P, PACK, WIDTH], F32) for matrix in matrices}
+        hidden_scales = [sbuf("hs%d" % e, [P, C], U8) for e in range(E)]
+        result = sbuf("res", [P, PACK, T], F32)
+        result_rounded = sbuf("resb", [P, T, PACK], BF16)
+        result_codes = sbuf("rq", [P, T], U32)
+        result_scales = sbuf("rs", [P, T], U8)
+        rounded = {}
+        deal_codes = {}
+        deal_scales = {}
+        slot_words = {}
+        slot_scales = {}
+        hidden_codes = {}
+        copied = {}
+        windows = {}
+
+        def entries(e, lo, hi):
+            return offsets[:, (e * C + lo) // PER_COLUMN:(e * C + hi) // PER_COLUMN]
+
+        def load_words(s):
+            words = x_words[s].rearrange("p t d -> p (t d)")
+            nc.sync.dma_start(out=token_words[s][:].bitcast(I32), in_=words.bitcast(I32))
 
         def load_matrix(e, m):
-            rows = w1[e, m * PASS:(m + 1) * PASS, :] if m < PASSES else w2[e]
-            nc.sync.dma_start(out=raw[e, m][:], in_=rows.rearrange("(p j) c -> p j c", j=PACK))
+            rows = w2[e] if m == SECOND else w1[e, m * PASS:(m + 1) * PASS, :]
+            nc.sync.dma_start(out=loaded[e, m][:], in_=rows.rearrange("(p j) c -> p j c", j=PACK))
 
-        def label(key, lo, hi):
-            return "%d%d" % key if hi - lo == PACK else "%d%d%d" % (key + (lo // 2,))
+        def label(matrix, lo, hi):
+            return "%d%d" % matrix if hi - lo == PACK else "%d%d%d" % (matrix + (lo // PAIR,))
 
-        def cast(key, lo, hi, on_vector):
-            name = label(key, lo, hi)
-            grouped[name] = sb("grp" + name, [P, hi - lo, P, PACK], BF16)
-            src = raw[key][:].rearrange("p j (m t) -> p m j t", t=PACK)[:, :, :, lo:hi]
-            dst = grouped[name][:].rearrange("p t m j -> p m j t")
-            if on_vector:
-                nc.vector.tensor_copy(out=dst, in_=src)
-            else:
-                nc.scalar.copy(out=dst, in_=src)
+        def round_deals(matrix, lo, hi, copy):
+            name = label(matrix, lo, hi)
+            rounded[name] = sbuf("grp" + name, [P, hi - lo, P, PACK], BF16)
+            src = loaded[matrix][:].rearrange("p (h l) (m t) -> p m h t l", l=2, t=PACK)[:, :, :, lo:hi, :]
+            copy(out=rounded[name][:].rearrange("p t m (h l) -> p m h t l", l=2), in_=src)
 
-        def quantise(key, lo, hi):
-            name = label(key, lo, hi)
-            source = grouped[name][:] if name in grouped else grouped["%d%d" % key][:, lo:hi, :, :]
-            codes = sb("wq" + name, [P, (hi - lo) * P], U32)
-            scales = sb("wsc" + name, [P, (hi - lo) * P], U8)
+        def quantise_deals(matrix, lo, hi):
+            name = label(matrix, lo, hi)
+            source = rounded[name][:] if name in rounded else rounded[label(matrix, 0, PACK)][:, lo:hi, :, :]
+            codes = sbuf("wq" + name, [P, (hi - lo) * P], U32)
+            scales = sbuf("wsc" + name, [P, (hi - lo) * P], U8)
             nc.vector.quantize_mx(
                 out=codes[:].bitcast(FP8X4),
                 scales=scales[:],
@@ -103,207 +127,206 @@ def tile_moe_ogt_silu_silu_kernel(
             )
             for t in range(lo, hi):
                 cols = slice((t - lo) * P, (t - lo + 1) * P)
-                wq[key + (t,)] = codes[:, cols].bitcast(FP8X4)
-                wsc[key + (t,)] = scales[:, cols]
-
-        def load_words(s):
-            nc.sync.dma_start(out=xw[s][:].bitcast(I32), in_=x_words[s].rearrange("p t d -> p (t d)").bitcast(I32))
+                deal_codes[matrix + (t,)] = codes[:, cols].bitcast(FP8X4)
+                deal_scales[matrix + (t,)] = scales[:, cols]
 
         def gather_words(e, s):
-            gw[e, s] = sb("gw%d%d" % (e, s), [P, C], U32)
-            nc.vector.tensor_copy(gw[e, s][:], xw[s][:].indirect(offsets[:, e * COLS:(e + 1) * COLS]))
+            slot_words[e, s] = sbuf("gw%d%d" % (e, s), [P, C], U32)
+            nc.vector.tensor_copy(slot_words[e, s][:], token_words[s][:].indirect(entries(e, 0, C)))
 
         def gather_scales(e):
-            gs[e] = sb("gs%d" % e, [P, C], U8)
-            nc.vector.tensor_copy(gs[e][:], xs[:].indirect(offsets[:, e * COLS:(e + 1) * COLS]))
+            slot_scales[e] = sbuf("gs%d" % e, [P, C], U8)
+            nc.vector.tensor_copy(slot_scales[e][:], token_scales[:].indirect(entries(e, 0, C)))
 
-        def layer1(e):
-            banks = [psum.tile([P, PACK, P], F32, name="hbank", tag="bank%d" % c) for c in range(2)]
-            for c in range(2):
+        def first_layer(e):
+            banks = [bank_tile("hbank", [P, PACK, P], c) for c in range(CHUNKS)]
+            for c in range(CHUNKS):
                 slots = slice(c * P, (c + 1) * P)
                 for t in range(PACK):
                     for s in range(PASSES):
                         nc.tensor.matmul_mx(
                             out=banks[c][:, t, :],
-                            lhsT=wq[e, s, t],
-                            lhsT_scale=wsc[e, s, t],
-                            rhs=gw[e, s][:, slots].bitcast(FP8X4),
-                            rhs_scale=gs[e][4 * s:P, slots],
+                            lhsT=deal_codes[e, s, t],
+                            lhsT_scale=deal_scales[e, s, t],
+                            rhs=slot_words[e, s][:, slots].bitcast(FP8X4),
+                            rhs_scale=slot_scales[e][SCALE_ROWS * s:P, slots],
                             start=(s == 0),
                             stop=(s == PASSES - 1),
                         )
             return banks
 
-        def hidden(e, c, banks):
+        def quantise_hidden(e, c, banks):
             slots = slice(c * P, (c + 1) * P)
-            hb = sb("hb%d%d" % (e, c), [P, P, PACK], BF16)
+            hidden = sbuf("hb%d%d" % (e, c), [P, P, PACK], BF16)
             if c == 0:
-                hq[e] = sb("hq%d" % e, [P, C], U32)
+                hidden_codes[e] = sbuf("hq%d" % e, [P, C], U32)
             nc.scalar.activation(
-                out=hb[:].rearrange("p (c i) t -> p c t i", i=2),
-                in_=banks[c][:].rearrange("p t (c i) -> p c t i", i=2),
+                out=hidden[:].rearrange("p (u i) t -> p u t i", i=2),
+                in_=banks[c][:].rearrange("p t (u i) -> p u t i", i=2),
                 func=SILU,
             )
             nc.vector.quantize_mx(
-                out=hq[e][:, slots].bitcast(FP8X4),
-                scales=hs[e][:, slots],
-                in_=hb[:].rearrange("p n t -> p (n t)"),
+                out=hidden_codes[e][:, slots].bitcast(FP8X4),
+                scales=hidden_scales[e][:, slots],
+                in_=hidden[:].rearrange("p n t -> p (n t)"),
             )
 
-        def layer2(e, t, where, lo=0, hi=C):
-            bank = psum.tile([P, hi - lo], F32, name="ybank", tag="bank%d" % where)
+        def second_layer(e, t, bank, lo, hi):
+            sums = bank_tile("ybank", [P, hi - lo], bank)
             nc.tensor.matmul_mx(
-                out=bank[:],
-                lhsT=wq[e, PASSES, t],
-                lhsT_scale=wsc[e, PASSES, t],
-                rhs=hq[e][:, lo:hi].bitcast(FP8X4),
-                rhs_scale=hs[e][:, lo:hi],
+                out=sums[:],
+                lhsT=deal_codes[e, SECOND, t],
+                lhsT_scale=deal_scales[e, SECOND, t],
+                rhs=hidden_codes[e][:, lo:hi].bitcast(FP8X4),
+                rhs_scale=hidden_scales[e][:, lo:hi],
                 start=True,
                 stop=True,
             )
-            return bank
+            return sums
 
-        def copy_out(e, t, bank, lo=0, hi=C):
-            ys[e, t, lo] = sb("y%d%d%d" % (e, t, lo), [P, hi - lo], F32)
-            nc.scalar.copy(out=ys[e, t, lo][:], in_=bank)
+        def copy_out(e, t, sums, lo, hi):
+            copied[e, t, lo] = sbuf("y%d%d%d" % (e, t, lo), [P, hi - lo], F32)
+            nc.scalar.copy(out=copied[e, t, lo][:], in_=sums)
 
-        def rows(e, t, where, lo=0, hi=C):
-            copy_out(e, t, layer2(e, t, where, lo, hi)[:], lo, hi)
+        def scatter(e, t, lo, hi):
+            window = windows[t][:].indirect(entries(e, lo, hi))
+            nc.vector.tensor_tensor(window, copied[e, t, lo][:], slot_weights[e][:, lo:hi], MULT)
 
-        def scatter(e, t, lo=0, hi=C):
-            lst = offsets[:, (e * C + lo) // 16:(e * C + hi) // 16]
-            nc.vector.tensor_tensor(comb[t][:].indirect(lst), ys[e, t, lo][:], gates[e][:, lo:hi], MULT)
+        def send_back(e, t, bank, lo, hi):
+            copy_out(e, t, second_layer(e, t, bank, lo, hi)[:], lo, hi)
+            scatter(e, t, lo, hi)
 
-        nc.vector.memset(xs[:].bitcast(I32), 0)
-        nc.gpsimd.memset(xs1[:].bitcast(I32), 0)
-        nc.gpsimd.memset(wgs[:].bitcast(I32), 0)
-        make_identity(nc, ident[:])
+        def send_back_first_pair(e):
+            for c in range(CHUNKS):
+                for t in range(PAIR):
+                    send_back(e, t, CHUNKS + PAIR * c + t, c * P, (c + 1) * P)
+
+        nc.vector.memset(token_scales[:].bitcast(I32), 0)
+        nc.gpsimd.memset(second_pass_scales[:].bitcast(I32), 0)
+        nc.gpsimd.memset(gate_scales[:].bitcast(I32), 0)
+        make_identity(nc, identity[:])
+        quadrants = [(QUADRANT * q, slice(SCALE_ROWS * q, SCALE_ROWS * (q + 1))) for q in range(P // QUADRANT)]
         nc.sync.dma_start(offsets[:], offs)
         load_words(0)
-        for q in range(QUADS):
+        for first, blocks in quadrants:
             nc.sync.dma_start(
-                out=xs[32 * q:32 * q + 4 * PASSES, :].bitcast(I32), in_=x_scales[:, 4 * q:4 * q + 4, :].bitcast(I32)
+                out=token_scales[first:first + SCALE_ROWS * PASSES, :].bitcast(I32),
+                in_=x_scales[:, blocks, :].bitcast(I32),
             )
         load_matrix(0, 0)
         load_matrix(0, 1)
         load_words(1)
-        load_matrix(0, 2)
-        nc.sync.dma_start(out=gates[0][:], in_=gate[:, 0:C])
+        load_matrix(0, SECOND)
+        nc.sync.dma_start(out=slot_weights[0][:], in_=gate[:, 0:C])
         for m in range(PASSES + 1):
             load_matrix(1, m)
-        nc.sync.dma_start(out=gates[1][:], in_=gate[:, C:2 * C])
-        nc.sync.dma_start(out=wgw[:].bitcast(I32), in_=wg_words.rearrange("s p c -> p s c").bitcast(I32))
-        for q in range(QUADS):
+        nc.sync.dma_start(out=slot_weights[1][:], in_=gate[:, C:2 * C])
+        nc.sync.dma_start(out=gate_words[:].bitcast(I32), in_=wg_words.rearrange("s p c -> p s c").bitcast(I32))
+        for first, blocks in quadrants:
             nc.sync.dma_start(
-                out=wgs[32 * q:32 * q + 4, :, :].bitcast(I32),
-                in_=wg_scales[:, 4 * q:4 * q + 4, :].rearrange("s r c -> r s c").bitcast(I32),
+                out=gate_scales[first:first + SCALE_ROWS, :, :].bitcast(I32),
+                in_=wg_scales[:, blocks, :].rearrange("s r c -> r s c").bitcast(I32),
             )
             nc.sync.dma_start(
-                out=xs1[32 * q:32 * q + 4, :].bitcast(I32), in_=x_scales[1, 4 * q:4 * q + 4, :].bitcast(I32)
+                out=second_pass_scales[first:first + SCALE_ROWS, :].bitcast(I32),
+                in_=x_scales[1, blocks, :].bitcast(I32),
             )
 
-        gather_words(0, 0)
-        gather_scales(0)
-        gather_words(1, 0)
-        gather_scales(1)
-        cast((0, 0), 0, 2, True)
-        cast((0, 0), 2, 4, False)
-        quantise((0, 0), 0, 2)
-        quantise((0, 0), 2, 4)
-        cast((0, 1), 0, 2, True)
-        cast((0, 1), 2, 4, False)
+        on_vector, on_scalar = nc.vector.tensor_copy, nc.scalar.copy
+        for e in range(E):
+            gather_words(e, 0)
+            gather_scales(e)
+        round_deals((0, 0), 0, PAIR, on_vector)
+        round_deals((0, 0), PAIR, PACK, on_scalar)
+        quantise_deals((0, 0), 0, PAIR)
+        quantise_deals((0, 0), PAIR, PACK)
+        round_deals((0, 1), 0, PAIR, on_vector)
+        round_deals((0, 1), PAIR, PACK, on_scalar)
         gather_words(0, 1)
-        quantise((0, 1), 0, 2)
-        quantise((0, 1), 2, 4)
+        quantise_deals((0, 1), 0, PAIR)
+        quantise_deals((0, 1), PAIR, PACK)
         gather_words(1, 1)
-        cast((0, 2), 0, 4, True)
-        quantise((0, 2), 0, 2)
-        banks = layer1(0)
-        hidden(0, 0, banks)
-        quantise((0, 2), 2, 4)
-        hidden(0, 1, banks)
-        for t in range(2):
-            comb[t] = sb("comb%d" % t, [P, T], F32)
-        for c in range(2):
-            for t in range(2):
-                rows(0, t, 2 + 2 * c + t, c * P, (c + 1) * P)
-                scatter(0, t, c * P, (c + 1) * P)
+        round_deals((0, SECOND), 0, PACK, on_vector)
+        quantise_deals((0, SECOND), 0, PAIR)
+        banks = first_layer(0)
+        quantise_hidden(0, 0, banks)
+        quantise_deals((0, SECOND), PAIR, PACK)
+        quantise_hidden(0, 1, banks)
+        for t in range(PAIR):
+            windows[t] = sbuf("comb%d" % t, [P, T], F32)
+        send_back_first_pair(0)
 
-        cast((1, 0), 0, 4, False)
-        second = layer2(0, 2, 1)
-        last = layer2(0, 3, 2)
-        quantise((1, 0), 0, 4)
-        cast((1, 1), 0, 2, False)
-        cast((1, 1), 2, 4, True)
-        quantise((1, 1), 0, 2)
-        quantise((1, 1), 2, 4)
-        copy_out(0, 2, second[:])
-        copy_out(0, 3, last[:, 0:P], 0, P)
-        for t in range(2, PACK):
-            comb[t] = sb("comb%d" % t, [P, T], F32)
-        scatter(0, 2)
+        round_deals((1, 0), 0, PACK, on_scalar)
+        deal_2 = second_layer(0, 2, 1, 0, C)
+        deal_3 = second_layer(0, 3, 2, 0, C)
+        quantise_deals((1, 0), 0, PACK)
+        round_deals((1, 1), 0, PAIR, on_scalar)
+        round_deals((1, 1), PAIR, PACK, on_vector)
+        quantise_deals((1, 1), 0, PAIR)
+        quantise_deals((1, 1), PAIR, PACK)
+        copy_out(0, 2, deal_2[:], 0, C)
+        copy_out(0, 3, deal_3[:, 0:P], 0, P)
+        for t in range(PAIR, PACK):
+            windows[t] = sbuf("comb%d" % t, [P, T], F32)
+        scatter(0, 2, 0, C)
         scatter(0, 3, 0, P)
-        cast((1, 2), 0, 4, False)
-        quantise((1, 2), 0, 4)
-        banks = layer1(1)
-        hidden(1, 0, banks)
-        copy_out(0, 3, last[:, P:C], P, C)
+        round_deals((1, SECOND), 0, PACK, on_scalar)
+        quantise_deals((1, SECOND), 0, PACK)
+        banks = first_layer(1)
+        quantise_hidden(1, 0, banks)
+        copy_out(0, 3, deal_3[:, P:C], P, C)
         scatter(0, 3, P, C)
-        hidden(1, 1, banks)
-        for c in range(2):
-            for t in range(2):
-                rows(1, t, 2 + 2 * c + t, c * P, (c + 1) * P)
-                scatter(1, t, c * P, (c + 1) * P)
-        for t in range(2, PACK):
-            rows(1, t, 4 + t)
-            scatter(1, t)
+        quantise_hidden(1, 1, banks)
+        send_back_first_pair(1)
+        for t in range(PAIR, PACK):
+            send_back(1, t, PACK + t, 0, C)
 
-        obanks = [psum.tile([P, T], F32, name="obank%d" % t, tag="bank%d" % (4 + t)) for t in range(PACK)]
+        gate_banks = [bank_tile("obank%d" % t, [P, T], PACK + t) for t in range(PACK)]
+        stationary_scales = [token_scales, second_pass_scales]
         for c in range(T // P):
-            toks = slice(c * P, (c + 1) * P)
-            bank = psum.tile([P, N], F32, name="gbank", tag="bank%d" % c)
+            tokens = slice(c * P, (c + 1) * P)
+            sums = bank_tile("gbank", [P, N], c)
             for s in range(PASSES):
                 nc.tensor.matmul_mx(
-                    out=bank[:],
-                    lhsT=xw[s][:, toks].bitcast(FP8X4),
-                    lhsT_scale=(xs if s == 0 else xs1)[:, toks],
-                    rhs=wgw[:, s, :].bitcast(FP4X4),
-                    rhs_scale=wgs[:, s, :],
+                    out=sums[:],
+                    lhsT=token_words[s][:, tokens].bitcast(FP8X4),
+                    lhsT_scale=stationary_scales[s][:, tokens],
+                    rhs=gate_words[:, s, :].bitcast(FP4X4),
+                    rhs_scale=gate_scales[:, s, :],
                     start=(s == 0),
                     stop=(s == PASSES - 1),
                 )
-            ot = sb("ot%d" % c, [P, PACK, P], F32)
+            dealt = sbuf("ot%d" % c, [P, PACK, P], F32)
             nc.scalar.activation(
-                out=ot[:].rearrange("p (h l) m -> p h m l", l=2),
-                in_=bank[:].rearrange("p (m h l) -> p h m l", h=2, l=2),
+                out=dealt[:].rearrange("p (h l) m -> p h m l", l=2),
+                in_=sums[:].rearrange("p (m h l) -> p h m l", h=2, l=2),
                 func=SILU,
             )
             for t in range(PACK):
-                nc.tensor.transpose(obanks[t][:, toks], ot[:, t, :], ident[:])
+                nc.tensor.transpose(gate_banks[t][:, tokens], dealt[:, t, :], identity[:])
 
+        halves = [slice(0, HALF), slice(HALF, T)]
         out_rows = out_0.rearrange("(p t) c -> p t c", t=PACK)
-        for half in range(2):
-            toks = slice(half * 256, half * 256 + 256)
+        for tokens in halves:
             for t in range(PACK):
-                nc.vector.tensor_tensor(res[:, t, toks], obanks[t][:, toks], comb[t][:, toks], MULT)
-            nc.sync.dma_start(out=out_rows[:, :, toks], in_=res[:, :, toks])
+                nc.vector.tensor_tensor(result[:, t, tokens], gate_banks[t][:, tokens], windows[t][:, tokens], MULT)
+            nc.sync.dma_start(out=out_rows[:, :, tokens], in_=result[:, :, tokens])
 
-        words = out_1[0].rearrange("p c d -> p (c d)").bitcast(I32)
-        halves = [slice(half * 256, half * 256 + 256) for half in range(2)]
-        for toks, copy in zip(halves, (nc.scalar.copy, nc.vector.tensor_copy)):
+        for tokens, copy in zip(halves, (on_scalar, on_vector)):
             copy(
-                out=resb[:, toks, :].rearrange("p (c i) t -> p c t i", i=4),
-                in_=res[:, :, toks].rearrange("p t (c i) -> p c t i", i=4),
+                out=result_rounded[:, tokens, :].rearrange("p (u i) t -> p u t i", i=4),
+                in_=result[:, :, tokens].rearrange("p t (u i) -> p u t i", i=4),
             )
-        for toks in halves:
+        out_words = out_1[0].rearrange("p c d -> p (c d)").bitcast(I32)
+        for tokens in halves:
             nc.vector.quantize_mx(
-                out=rq[:, toks].bitcast(FP8X4),
-                scales=rs[:, toks],
-                in_=resb[:, toks, :].rearrange("p c t -> p (c t)"),
+                out=result_codes[:, tokens].bitcast(FP8X4),
+                scales=result_scales[:, tokens],
+                in_=result_rounded[:, tokens, :].rearrange("p c t -> p (c t)"),
             )
-            nc.sync.dma_start(out=words[:, toks], in_=rq[:, toks].bitcast(I32))
-        for q in range(QUADS):
-            queue = nc.sync if q % 2 == 0 else nc.scalar
+            nc.sync.dma_start(out=out_words[:, tokens], in_=result_codes[:, tokens].bitcast(I32))
+        for (first, blocks), queue in zip(quadrants, (nc.sync, nc.scalar, nc.sync, nc.scalar)):
             queue.dma_start(
-                out=out_2[0, 4 * q:4 * q + 4, :].bitcast(I32), in_=rs[32 * q:32 * q + 4, :].bitcast(I32)
+                out=out_2[0, blocks, :].bitcast(I32),
+                in_=result_scales[first:first + SCALE_ROWS, :].bitcast(I32),
             )

from contextlib import ExitStack

import concourse.mybir as mybir
from concourse.masks import make_identity

K, T, E, C, H, N = 1024, 512, 2, 256, 512, 512
FLOPS = 2 * K * N * T + 2 * K * H * E * C + 2 * H * N * E * C

F32 = mybir.dt.float32
BF16 = mybir.dt.bfloat16
I32 = mybir.dt.int32
U32 = mybir.dt.uint32
U16 = mybir.dt.uint16
U8 = mybir.dt.uint8
FP8X4 = mybir.dt.float8_e4m3fn_x4
FP4X4 = mybir.dt.float4_e2m1fn_x4
SILU = mybir.ActivationFunctionType.Silu
MULT = mybir.AluOpType.mult

P = 128
PACK = 4
PASS = P * PACK
PASSES = K // PASS
SECOND = PASSES
WIDTH = 512
PAIR = PACK // 2
QUADRANT = 32
SCALE_ROWS = 4
PER_COLUMN = 16
CHUNKS = C // P
HALF = T // 2
KIB = 1024

SHARED = {
    "grp011": 0,
    "gw11": 0,
    "grp02": 1 * KIB,
    "wq020": 5 * KIB,
    "grp10": 5 * KIB,
    "raw10": 16 * KIB,
    "grp111": 18 * KIB,
    "raw11": 24 * KIB,
    "comb2": 24 * KIB,
    "y020": 26 * KIB,
    "y030": 27 * KIB,
    "raw12": 32 * KIB,
    "y03128": 34 * KIB,
    "hb11": 40 * KIB,
    "ot0": 40 * KIB,
    "raw02": 42 * KIB,
    "hq0": 42 * KIB,
    "grp110": 42 * KIB,
    "grp12": 42 * KIB,
}


def tile_moe_ogt_silu_silu_kernel(
    tc, x_words, x_scales, wg_words, wg_scales, w1, w2, gate, offs, out_0, out_1, out_2
):
    nc = tc.nc
    with ExitStack() as ctx:
        keep = ctx.enter_context(tc.tile_pool(name="keep", bufs=1))
        shared = ctx.enter_context(tc.tile_pool(name="lap", bufs=1))
        psum = ctx.enter_context(tc.psum_pool(name="psum", bufs=1))

        def sbuf(name, shape, dtype):
            if name in SHARED:
                return shared.tile(shape, dtype, name=name, tag=name, align_bytes=64, offset=SHARED[name])
            return keep.tile(shape, dtype, name=name, tag=name, align_bytes=64)

        def bank_tile(name, shape, bank):
            return psum.tile(shape, F32, name=name, tag="bank%d" % bank)

        offsets = keep.tile([P, E * C // PER_COLUMN], U16, name="offsets")
        token_words = [sbuf("xw%d" % s, [P, T], U32) for s in range(PASSES)]
        token_scales = sbuf("xs", [P, T], U8)
        second_pass_scales = sbuf("xs1", [P, T], U8)
        gate_words = sbuf("wgw", [P, PASSES, 2 * N], U8)
        gate_scales = sbuf("wgs", [P, PASSES, N], U8)
        slot_weights = [sbuf("gate%d" % e, [P, C], F32) for e in range(E)]
        identity = sbuf("ident", [P, P], F32)
        matrices = [(e, m) for e in range(E) for m in range(PASSES + 1)]
        loaded = {matrix: sbuf("raw%d%d" % matrix, [P, PACK, WIDTH], F32) for matrix in matrices}
        hidden_scales = [sbuf("hs%d" % e, [P, C], U8) for e in range(E)]
        result = sbuf("res", [P, PACK, T], F32)
        result_rounded = sbuf("resb", [P, T, PACK], BF16)
        result_codes = sbuf("rq", [P, T], U32)
        result_scales = sbuf("rs", [P, T], U8)
        rounded = {}
        deal_codes = {}
        deal_scales = {}
        slot_words = {}
        slot_scales = {}
        hidden_codes = {}
        copied = {}
        windows = {}

        def entries(e, lo, hi):
            return offsets[:, (e * C + lo) // PER_COLUMN:(e * C + hi) // PER_COLUMN]

        def load_words(s):
            words = x_words[s].rearrange("p t d -> p (t d)")
            nc.sync.dma_start(out=token_words[s][:].bitcast(I32), in_=words.bitcast(I32))

        def load_matrix(e, m):
            rows = w2[e] if m == SECOND else w1[e, m * PASS:(m + 1) * PASS, :]
            nc.sync.dma_start(out=loaded[e, m][:], in_=rows.rearrange("(p j) c -> p j c", j=PACK))

        def label(matrix, lo, hi):
            return "%d%d" % matrix if hi - lo == PACK else "%d%d%d" % (matrix + (lo // PAIR,))

        def round_deals(matrix, lo, hi, copy):
            name = label(matrix, lo, hi)
            rounded[name] = sbuf("grp" + name, [P, hi - lo, P, PACK], BF16)
            src = loaded[matrix][:].rearrange("p (h l) (m t) -> p m h t l", l=2, t=PACK)[:, :, :, lo:hi, :]
            copy(out=rounded[name][:].rearrange("p t m (h l) -> p m h t l", l=2), in_=src)

        def quantise_deals(matrix, lo, hi):
            name = label(matrix, lo, hi)
            source = rounded[name][:] if name in rounded else rounded[label(matrix, 0, PACK)][:, lo:hi, :, :]
            codes = sbuf("wq" + name, [P, (hi - lo) * P], U32)
            scales = sbuf("wsc" + name, [P, (hi - lo) * P], U8)
            nc.vector.quantize_mx(
                out=codes[:].bitcast(FP8X4),
                scales=scales[:],
                in_=source.rearrange("p t m j -> p (t m j)"),
            )
            for t in range(lo, hi):
                cols = slice((t - lo) * P, (t - lo + 1) * P)
                deal_codes[matrix + (t,)] = codes[:, cols].bitcast(FP8X4)
                deal_scales[matrix + (t,)] = scales[:, cols]

        def gather_words(e, s):
            slot_words[e, s] = sbuf("gw%d%d" % (e, s), [P, C], U32)
            nc.vector.tensor_copy(slot_words[e, s][:], token_words[s][:].indirect(entries(e, 0, C)))

        def gather_scales(e):
            slot_scales[e] = sbuf("gs%d" % e, [P, C], U8)
            nc.vector.tensor_copy(slot_scales[e][:], token_scales[:].indirect(entries(e, 0, C)))

        def first_layer(e):
            banks = [bank_tile("hbank", [P, PACK, P], c) for c in range(CHUNKS)]
            for c in range(CHUNKS):
                slots = slice(c * P, (c + 1) * P)
                for t in range(PACK):
                    for s in range(PASSES):
                        nc.tensor.matmul_mx(
                            out=banks[c][:, t, :],
                            lhsT=deal_codes[e, s, t],
                            lhsT_scale=deal_scales[e, s, t],
                            rhs=slot_words[e, s][:, slots].bitcast(FP8X4),
                            rhs_scale=slot_scales[e][SCALE_ROWS * s:P, slots],
                            start=(s == 0),
                            stop=(s == PASSES - 1),
                        )
            return banks

        def quantise_hidden(e, c, banks):
            slots = slice(c * P, (c + 1) * P)
            hidden = sbuf("hb%d%d" % (e, c), [P, P, PACK], BF16)
            if c == 0:
                hidden_codes[e] = sbuf("hq%d" % e, [P, C], U32)
            nc.scalar.activation(
                out=hidden[:].rearrange("p (u i) t -> p u t i", i=2),
                in_=banks[c][:].rearrange("p t (u i) -> p u t i", i=2),
                func=SILU,
            )
            nc.vector.quantize_mx(
                out=hidden_codes[e][:, slots].bitcast(FP8X4),
                scales=hidden_scales[e][:, slots],
                in_=hidden[:].rearrange("p n t -> p (n t)"),
            )

        def second_layer(e, t, bank, lo, hi):
            sums = bank_tile("ybank", [P, hi - lo], bank)
            nc.tensor.matmul_mx(
                out=sums[:],
                lhsT=deal_codes[e, SECOND, t],
                lhsT_scale=deal_scales[e, SECOND, t],
                rhs=hidden_codes[e][:, lo:hi].bitcast(FP8X4),
                rhs_scale=hidden_scales[e][:, lo:hi],
                start=True,
                stop=True,
            )
            return sums

        def copy_out(e, t, sums, lo, hi):
            copied[e, t, lo] = sbuf("y%d%d%d" % (e, t, lo), [P, hi - lo], F32)
            nc.scalar.copy(out=copied[e, t, lo][:], in_=sums)

        def scatter(e, t, lo, hi):
            window = windows[t][:].indirect(entries(e, lo, hi))
            nc.vector.tensor_tensor(window, copied[e, t, lo][:], slot_weights[e][:, lo:hi], MULT)

        def send_back(e, t, bank, lo, hi):
            copy_out(e, t, second_layer(e, t, bank, lo, hi)[:], lo, hi)
            scatter(e, t, lo, hi)

        def send_back_first_pair(e):
            for c in range(CHUNKS):
                for t in range(PAIR):
                    send_back(e, t, CHUNKS + PAIR * c + t, c * P, (c + 1) * P)

        nc.vector.memset(token_scales[:].bitcast(I32), 0)
        nc.gpsimd.memset(second_pass_scales[:].bitcast(I32), 0)
        nc.gpsimd.memset(gate_scales[:].bitcast(I32), 0)
        make_identity(nc, identity[:])
        quadrants = [(QUADRANT * q, slice(SCALE_ROWS * q, SCALE_ROWS * (q + 1))) for q in range(P // QUADRANT)]
        nc.sync.dma_start(offsets[:], offs)
        load_words(0)
        for first, blocks in quadrants:
            nc.sync.dma_start(
                out=token_scales[first:first + SCALE_ROWS * PASSES, :].bitcast(I32),
                in_=x_scales[:, blocks, :].bitcast(I32),
            )
        load_matrix(0, 0)
        load_matrix(0, 1)
        load_words(1)
        load_matrix(0, SECOND)
        nc.sync.dma_start(out=slot_weights[0][:], in_=gate[:, 0:C])
        for m in range(PASSES + 1):
            load_matrix(1, m)
        nc.sync.dma_start(out=slot_weights[1][:], in_=gate[:, C:2 * C])
        nc.sync.dma_start(out=gate_words[:].bitcast(I32), in_=wg_words.rearrange("s p c -> p s c").bitcast(I32))
        for first, blocks in quadrants:
            nc.sync.dma_start(
                out=gate_scales[first:first + SCALE_ROWS, :, :].bitcast(I32),
                in_=wg_scales[:, blocks, :].rearrange("s r c -> r s c").bitcast(I32),
            )
            nc.sync.dma_start(
                out=second_pass_scales[first:first + SCALE_ROWS, :].bitcast(I32),
                in_=x_scales[1, blocks, :].bitcast(I32),
            )

        on_vector, on_scalar = nc.vector.tensor_copy, nc.scalar.copy
        for e in range(E):
            gather_words(e, 0)
            gather_scales(e)
        round_deals((0, 0), 0, PAIR, on_vector)
        round_deals((0, 0), PAIR, PACK, on_scalar)
        quantise_deals((0, 0), 0, PAIR)
        quantise_deals((0, 0), PAIR, PACK)
        round_deals((0, 1), 0, PAIR, on_vector)
        round_deals((0, 1), PAIR, PACK, on_scalar)
        gather_words(0, 1)
        quantise_deals((0, 1), 0, PAIR)
        quantise_deals((0, 1), PAIR, PACK)
        gather_words(1, 1)
        round_deals((0, SECOND), 0, PACK, on_vector)
        quantise_deals((0, SECOND), 0, PAIR)
        banks = first_layer(0)
        quantise_hidden(0, 0, banks)
        quantise_deals((0, SECOND), PAIR, PACK)
        quantise_hidden(0, 1, banks)
        for t in range(PAIR):
            windows[t] = sbuf("comb%d" % t, [P, T], F32)
        send_back_first_pair(0)

        round_deals((1, 0), 0, PACK, on_scalar)
        deal_2 = second_layer(0, 2, 1, 0, C)
        deal_3 = second_layer(0, 3, 2, 0, C)
        quantise_deals((1, 0), 0, PACK)
        round_deals((1, 1), 0, PAIR, on_scalar)
        round_deals((1, 1), PAIR, PACK, on_vector)
        quantise_deals((1, 1), 0, PAIR)
        quantise_deals((1, 1), PAIR, PACK)
        copy_out(0, 2, deal_2[:], 0, C)
        copy_out(0, 3, deal_3[:, 0:P], 0, P)
        for t in range(PAIR, PACK):
            windows[t] = sbuf("comb%d" % t, [P, T], F32)
        scatter(0, 2, 0, C)
        scatter(0, 3, 0, P)
        round_deals((1, SECOND), 0, PACK, on_scalar)
        quantise_deals((1, SECOND), 0, PACK)
        banks = first_layer(1)
        quantise_hidden(1, 0, banks)
        copy_out(0, 3, deal_3[:, P:C], P, C)
        scatter(0, 3, P, C)
        quantise_hidden(1, 1, banks)
        send_back_first_pair(1)
        for t in range(PAIR, PACK):
            send_back(1, t, PACK + t, 0, C)

        gate_banks = [bank_tile("obank%d" % t, [P, T], PACK + t) for t in range(PACK)]
        stationary_scales = [token_scales, second_pass_scales]
        for c in range(T // P):
            tokens = slice(c * P, (c + 1) * P)
            sums = bank_tile("gbank", [P, N], c)
            for s in range(PASSES):
                nc.tensor.matmul_mx(
                    out=sums[:],
                    lhsT=token_words[s][:, tokens].bitcast(FP8X4),
                    lhsT_scale=stationary_scales[s][:, tokens],
                    rhs=gate_words[:, s, :].bitcast(FP4X4),
                    rhs_scale=gate_scales[:, s, :],
                    start=(s == 0),
                    stop=(s == PASSES - 1),
                )
            dealt = sbuf("ot%d" % c, [P, PACK, P], F32)
            nc.scalar.activation(
                out=dealt[:].rearrange("p (h l) m -> p h m l", l=2),
                in_=sums[:].rearrange("p (m h l) -> p h m l", h=2, l=2),
                func=SILU,
            )
            for t in range(PACK):
                nc.tensor.transpose(gate_banks[t][:, tokens], dealt[:, t, :], identity[:])

        halves = [slice(0, HALF), slice(HALF, T)]
        out_rows = out_0.rearrange("(p t) c -> p t c", t=PACK)
        for tokens in halves:
            for t in range(PACK):
                nc.vector.tensor_tensor(result[:, t, tokens], gate_banks[t][:, tokens], windows[t][:, tokens], MULT)
            nc.sync.dma_start(out=out_rows[:, :, tokens], in_=result[:, :, tokens])

        for tokens, copy in zip(halves, (on_scalar, on_vector)):
            copy(
                out=result_rounded[:, tokens, :].rearrange("p (u i) t -> p u t i", i=4),
                in_=result[:, :, tokens].rearrange("p t (u i) -> p u t i", i=4),
            )
        out_words = out_1[0].rearrange("p c d -> p (c d)").bitcast(I32)
        for tokens in halves:
            nc.vector.quantize_mx(
                out=result_codes[:, tokens].bitcast(FP8X4),
                scales=result_scales[:, tokens],
                in_=result_rounded[:, tokens, :].rearrange("p c t -> p (c t)"),
            )
            nc.sync.dma_start(out=out_words[:, tokens], in_=result_codes[:, tokens].bitcast(I32))
        for (first, blocks), queue in zip(quadrants, (nc.sync, nc.scalar, nc.sync, nc.scalar)):
            queue.dma_start(
                out=out_2[0, blocks, :].bitcast(I32),
                in_=result_scales[first:first + SCALE_ROWS, :].bitcast(I32),
            )
